import numpy as np
import ml_dtypes


def mxq(x, axis, fmt="e4m3"):
    dtype, down = {"e4m3": (ml_dtypes.float8_e4m3fn, 7), "e5m2": (ml_dtypes.float8_e5m2, 14)}[fmt]
    v = np.moveaxis(np.asarray(x, np.float32).astype(ml_dtypes.bfloat16).astype(np.float64), axis, -1)
    blocks = v.reshape(v.shape[:-1] + (-1, 32))
    amax = np.abs(blocks).max(-1, keepdims=True)
    byte = np.maximum(np.where(amax > 0, np.frexp(amax)[1] - 1 + 127, 0) - down, 1)
    scale = np.exp2(byte - 127.0)
    codes = (blocks / scale).astype(np.float32).astype(dtype).astype(np.float64)
    return np.moveaxis((codes * scale).reshape(v.shape), -1, axis)


WIDE = False


def mx_kscale(k):
    if not WIDE:
        return np.ones(k)
    levels = np.array([10, -10, 5, -5, 0])
    if k % 512:
        return np.exp2(np.random.permutation(np.resize(levels, k // 32))).repeat(32)
    a = np.empty((k // 512, 16))
    for p in range(k // 512):
        a[p, :8] = np.random.permutation(np.resize(levels, 8))
        for g in range(8):
            far = levels[np.abs(levels - a[p, g]) >= 10]
            a[p, g + 8] = far[np.random.randint(len(far))]
    return np.exp2(a.ravel()).repeat(32)


def f64(x):
    return np.asarray(x).astype(np.float64)


def striped(idx):
    return np.tile(np.asarray(idx).reshape(-1, 16).T, (8, 1)).astype(np.uint16)


def unstriped(offs):
    return offs[:16].T.reshape(-1).astype(np.int64)


def striped8(idx):
    return np.asarray(idx).reshape(8, -1, 16).transpose(0, 2, 1).reshape(128, -1).astype(np.uint16)


def unstriped8(offs):
    return offs.reshape(8, 16, -1).transpose(0, 2, 1).reshape(8, -1).astype(np.int64)


def pick8(x, idx, run):
    r = np.arange(len(x))
    return x[r[:, None], idx[r % (8 * run) // run]]


E2M1 = np.array([0.0, 0.5, 1.0, 1.5, 2.0, 3.0, 4.0, 6.0, -0.0, -0.5, -1.0, -1.5, -2.0, -3.0, -4.0, -6.0])


def pack_weight(w, fmt):
    k, n = w.shape
    w = f64(np.asarray(w, np.float32).astype(ml_dtypes.bfloat16)).reshape(k // 32, 32, n)
    amax = np.abs(w).max(1)
    if fmt == "e4m3":
        byte = np.frexp(amax)[1] - 1 + 127 - 7
    else:
        mant, ex = np.frexp(amax / 6.0)
        byte = np.where(mant > 0.5, ex, ex - 1) + 127
    byte = np.clip(np.where(amax > 0, byte, 1), 1, 254)
    scaled = (w * np.exp2(127.0 - byte)[:, None, :]).reshape(k, n).astype(np.float32)
    by_word = np.ascontiguousarray(scaled.reshape(k // 512, 128, 4, n).transpose(0, 1, 3, 2))
    if fmt == "e4m3":
        words = by_word.astype(ml_dtypes.float8_e4m3fn).view(np.uint8)
    else:
        c = by_word.astype(ml_dtypes.float4_e2m1fn).view(np.uint8) & 0xF
        words = (c[..., 0::2] | (c[..., 1::2] << 4)).reshape(k // 512, 128, 2 * n)
    return np.ascontiguousarray(words), np.ascontiguousarray(byte.astype(np.uint8).reshape(k // 512, 16, n))


def unpack_weight(words, scales, fmt):
    g, _, n = scales.shape
    words = np.ascontiguousarray(words).reshape(g, 128, n, -1)
    if fmt == "e4m3":
        vals = words.view(ml_dtypes.float8_e4m3fn).astype(np.float64)
    else:
        nib = np.empty((g, 128, n, 4), np.uint8)
        nib[..., 0::2] = words & 0xF
        nib[..., 1::2] = words >> 4
        vals = E2M1[nib]
    vals = vals * np.repeat(np.exp2(scales.astype(np.float64) - 127.0), 8, axis=1)[..., None]
    return vals.transpose(0, 1, 3, 2).reshape(g * 512, n)


def sgn(shape):
    return np.random.uniform(0.5, 2.0, shape) * np.where(np.random.standard_normal(shape) < 0, -1.0, 1.0)


K, J, R, T, U, F, S, O, N, Z, W = 512, 512, 512, 1024, 1024, 1024, 256, 128, 256, 512, 512


def setup_inputs():
    n = np.random.standard_normal
    idx = np.stack([np.random.permutation(T)[:J] for _ in range(8)])
    idx2 = np.stack([np.random.permutation(U)[:J] for _ in range(8)])
    idx3 = np.random.permutation(F)[:R]
    idx4 = np.stack([np.random.permutation(J)[:S] for _ in range(8)])
    idx5 = np.random.permutation(J)[:S]
    idx6 = np.stack([np.random.permutation(Z)[:N] for _ in range(8)])
    idx7 = np.stack([np.random.permutation(W)[:N] for _ in range(8)])
    fk = mx_kscale(K)
    fr = mx_kscale(R)
    tr = np.ones(F)
    tr[idx3] = fr
    wtp = pack_weight(n((K, F)) * 1 / np.sqrt(K) / fk[:, None] * tr, "e2m1")
    return {
        "ta": (np.random.randint(-7, 8, (K, T)).astype(np.float64)).astype(np.float32),
        "tb": (np.random.randint(-7, 8, (K, U)).astype(np.float64)).astype(np.float32),
        "ga": ((np.random.randint(8, 25, (K, 1)) / 64.0) * fk[:, None]).astype(np.float32),
        "gb": ((np.random.randint(8, 25, (K, 1)) / 64.0) * fk[:, None]).astype(np.float32),
        "wt_words": wtp[0],
        "wt_scales": wtp[1],
        "sa": (sgn((R, 1))).astype(np.float32),
        "sb": (sgn((R, 1))).astype(np.float32),
        "va": (np.random.randint(-7, 8, (R, Z)).astype(np.float64)).astype(np.float32),
        "vb": (np.random.randint(-7, 8, (R, W)).astype(np.float64)).astype(np.float32),
        "ea": ((np.random.randint(10, 25, (R, 1)) / 1024.0) / fr[:, None]).astype(np.float32),
        "eb": ((np.random.randint(4, 13, (R, 1)) / 1024.0) / fr[:, None]).astype(np.float32),
        "offs": striped8(idx),
        "offs2": striped8(idx2),
        "offs3": striped(idx3),
        "offs4": striped8(idx4),
        "offs5": striped(idx5),
        "offs6": striped8(idx6),
        "offs7": striped8(idx7),
    }


def reference(ta, tb, ga, gb, wt_words, wt_scales, sa, sb, va, vb, ea, eb, offs, offs2, offs3, offs4, offs5, offs6, offs7):
    idx = unstriped8(offs)
    idx2 = unstriped8(offs2)
    idx3 = unstriped(offs3)
    idx4 = unstriped8(offs4)
    idx5 = unstriped(offs5)
    idx6 = unstriped8(offs6)
    idx7 = unstriped8(offs7)
    wtu = unpack_weight(wt_words, wt_scales, "e2m1")
    xc = np.maximum(pick8(f64(ta), idx, 64) * f64(ga), pick8(f64(tb), idx2, 64) * f64(gb))
    wtidx3g = wtu[:, idx3]
    xcq = mxq(xc, 0, "e4m3")
    a = wtidx3g.T @ xcq
    h1 = np.maximum(pick8(a, idx4, 64) * f64(sa), a[:, idx5] * f64(sb))
    hid = h1.reshape(R, O, S // O).max(axis=2)
    vc = pick8(f64(va), idx6, 64) * f64(ea) + pick8(f64(vb), idx7, 64) * f64(eb)
    vcq = mxq(vc, 0, "e4m3")
    hidq = mxq(hid, 0, "e4m3")
    y = vcq.T @ hidq
    return y

@@ -1,0 +1,175 @@
+from contextlib import ExitStack
+
+import concourse.mybir as mybir
+
+K, J, R, T, F, S, O, N, Z = 512, 512, 512, 1024, 1024, 256, 128, 256, 512
+FLOPS = 2 * K * R * J + 2 * R * N * O
+
+P = 128
+PACK = 4
+F32, BF16 = mybir.dt.float32, mybir.dt.bfloat16
+I32, U32, U16, U8 = mybir.dt.int32, mybir.dt.uint32, mybir.dt.uint16, mybir.dt.uint8
+FP8X4, FP4X4 = mybir.dt.float8_e4m3fn_x4, mybir.dt.float4_e2m1fn_x4
+COPY = mybir.ActivationFunctionType.Copy
+MAX, ADD = mybir.AluOpType.max, mybir.AluOpType.add
+
+
+def tile_picked_largercode_store_one_pooledgroups_twobooks_plain_kernel(
+    tc, ta, tb, ga, gb, wt_words, wt_scales, sa, sb, va, vb, ea, eb,
+    offs, offs2, offs3, offs4, offs5, offs6, offs7, out,
+):
+    nc = tc.nc
+    with ExitStack() as ctx:
+        keep = ctx.enter_context(tc.tile_pool(name="keep", bufs=1))
+        psum = ctx.enter_context(tc.psum_pool(name="psum", bufs=1))
+
+        def sbuf(name, shape, dtype, tag=None):
+            return keep.tile(shape, dtype, name=name, tag=tag or name, align_bytes=64)
+
+        def load_list(name, src):
+            tile = sbuf(name, list(src.shape), U16)
+            nc.sync.dma_start(tile[:], src)
+            return tile
+
+        def load_factor(queue, name, src):
+            tile = sbuf(name, [P, PACK], F32)
+            queue.dma_start(tile[:], src.rearrange("(p t) o -> p (t o)", t=PACK))
+            return tile
+
+        def load_plane(name, src, t):
+            tile = sbuf(f"{name}{t}", [P, src.shape[1]], F32)
+            nc.sync.dma_start(tile[:], src.rearrange("(p t) c -> p t c", t=PACK)[:, t, :])
+            return tile
+
+        def fetch(dst, window, offsets, factor, t):
+            nc.scalar.activation(dst, window[:].indirect(offsets), COPY, scale=factor[:, t : t + 1])
+
+        ta_w, tb_w, va_w, vb_w = [], [], [], []
+        l1 = load_list("l1", offs)
+        ga_t = load_factor(nc.scalar, "ga_t", ga)
+        gb_t = load_factor(nc.scalar, "gb_t", gb)
+        ta_w.append(load_plane("ta", ta, 0))
+        l2 = load_list("l2", offs2)
+        tb_w.append(load_plane("tb", tb, 0))
+        stage = sbuf("stage", [4, 4, F // 4], I32)
+        nc.gpsimd.dma_start(stage[:], wt_scales[0].bitcast(I32).rearrange("(q i) c -> i q c", i=4))
+        ea_t = load_factor(nc.gpsimd, "ea_t", ea)
+        eb_t = load_factor(nc.gpsimd, "eb_t", eb)
+        sa_t = load_factor(nc.gpsimd, "sa_t", sa)
+        sb_t = load_factor(nc.gpsimd, "sb_t", sb)
+        for t in (1, 2):
+            ta_w.append(load_plane("ta", ta, t))
+            tb_w.append(load_plane("tb", tb, t))
+        l3 = load_list("l3", offs3)
+        words_w = sbuf("words_w", [P, F], U16)
+        nc.sync.dma_start(words_w[:].bitcast(I32), wt_words[0].bitcast(I32))
+        ta_w.append(load_plane("ta", ta, 3))
+        tb_w.append(load_plane("tb", tb, 3))
+        l6 = load_list("l6", offs6)
+        l7 = load_list("l7", offs7)
+        for t in (0, 1):
+            va_w.append(load_plane("va", va, t))
+            vb_w.append(load_plane("vb", vb, t))
+        l4 = load_list("l4", offs4)
+        l5 = load_list("l5", offs5)
+        for t in (2, 3):
+            va_w.append(load_plane("va", va, t))
+            vb_w.append(load_plane("vb", vb, t))
+
+        scales_w = sbuf("scales_w", [P, F], U8)
+        nc.vector.memset(scales_w[:].bitcast(I32), 0)
+        for q in range(4):
+            nc.vector.tensor_copy(scales_w[32 * q : 32 * q + 4, :].bitcast(I32), stage[:, q, :])
+        w_scales = sbuf("w_scales", [P, PACK, P], U8)
+        nc.vector.tensor_copy(w_scales[:].rearrange("p t m -> p m t"), scales_w[:].indirect(l3[:]))
+        picked = sbuf("picked", [P, R], U16)
+        nc.vector.tensor_copy(picked[:], words_w[:].indirect(l3[:]))
+        w_words = sbuf("w_words", [P, PACK, P, 2], U8)
+        nc.vector.tensor_copy(
+            w_words[:], picked[:].bitcast(U8).rearrange("p (m t b) -> p t m b", t=PACK, b=2)
+        )
+
+        xa = sbuf("xa", [P, PACK, J], F32)
+        xb = sbuf("xb", [P, PACK, J], F32)
+        H = J // 2
+        for t in range(PACK):
+            fetch(xa[:, t, :], ta_w[t], l1[:], ga_t, t)
+            if t < PACK - 1:
+                fetch(xb[:, t, :], tb_w[t], l2[:], gb_t, t)
+            else:
+                for h in range(2):
+                    fetch(xb[:, t, h * H : (h + 1) * H], tb_w[t], l2[:, h * H // 16 : (h + 1) * H // 16], gb_t, t)
+
+        xc = sbuf("xc", [P, J, PACK], BF16)
+        x_codes = sbuf("x_codes", [P, J], U32)
+        x_scales = sbuf("x_scales", [P, J], U8)
+        a_ps = [psum.tile([P, J], F32, name=f"a_ps{t}") for t in range(PACK)]
+
+        def weave(dst, in0, in1, op):
+            nc.vector.tensor_tensor(
+                dst.rearrange("p (c i) t -> p c t i", i=2),
+                in0.rearrange("p t (c i) -> p c t i", i=2),
+                in1.rearrange("p t (c i) -> p c t i", i=2),
+                op,
+            )
+
+        for h in range(2):
+            cols = slice(h * H, (h + 1) * H)
+            weave(xc[:, cols, :], xa[:, :, cols], xb[:, :, cols], MAX)
+            nc.vector.quantize_mx(
+                out=x_codes[:, cols].bitcast(FP8X4), scales=x_scales[:, cols],
+                in_=xc[:, cols, :].rearrange("p j t -> p (j t)"),
+            )
+        for t in range(PACK):
+            nc.tensor.matmul_mx(
+                out=a_ps[t][:],
+                lhsT=w_words[:, t].rearrange("p m b -> p (m b)").bitcast(FP4X4),
+                lhsT_scale=w_scales[:, t, :],
+                rhs=x_codes[:].bitcast(FP8X4), rhs_scale=x_scales[:],
+                start=True, stop=True,
+            )
+        a_w = [sbuf(f"a_w{t}", [P, J], F32) for t in range(PACK)]
+        for t in range(PACK):
+            nc.vector.tensor_copy(a_w[t][:], a_ps[t][:])
+
+        ya = sbuf("ya", [P, PACK, N], F32)
+        yb = sbuf("yb", [P, PACK, N], F32)
+        for t in range(PACK):
+            fetch(ya[:, t, :], va_w[t], l6[:], ea_t, t)
+            fetch(yb[:, t, :], vb_w[t], l7[:], eb_t, t)
+        vc = sbuf("vc", [P, N, PACK], BF16)
+        v_codes = sbuf("v_codes", [P, N], U32)
+        v_scales = sbuf("v_scales", [P, N], U8)
+        weave(vc[:], ya[:], yb[:], ADD)
+        nc.vector.quantize_mx(out=v_codes[:].bitcast(FP8X4), scales=v_scales[:], in_=vc[:].rearrange("p n t -> p (n t)"))
+
+        hid = sbuf("hid", [P, O, PACK], BF16)
+        picks = sbuf("picks", [P, PACK, 2, S], F32, tag="vb3")
+        for t in range(PACK):
+            both = picks[:, t]
+            fetch(both[:, 0, :], a_w[t], l4[:], sa_t, t)
+            cuts = (0, S) if t < PACK - 1 else (0, S - 64, S)
+            for s0, s1 in zip(cuts, cuts[1:]):
+                fetch(both[:, 1, s0:s1], a_w[t], l5[:, s0 // 16 : s1 // 16], sb_t, t)
+                nc.vector.tensor_reduce(
+                    hid[:, s0 // 2 : s1 // 2, t], both[:, :, s0:s1].rearrange("p l (o d) -> p o l d", d=2),
+                    mybir.AxisListType.XY, MAX,
+                )
+        h_codes = sbuf("h_codes", [P, O], U32)
+        h_scales = sbuf("h_scales", [P, O], U8)
+        nc.vector.quantize_mx(out=h_codes[:].bitcast(FP8X4), scales=h_scales[:], in_=hid[:].rearrange("p o t -> p (o t)"))
+
+        for u in range(N // P):
+            rows = slice(u * P, (u + 1) * P)
+            y_ps = psum.tile([P, O], F32, name=f"y_ps{u}")
+            nc.tensor.matmul_mx(
+                out=y_ps[:], lhsT=v_codes[:, rows].bitcast(FP8X4), lhsT_scale=v_scales[:, rows],
+                rhs=h_codes[:].bitcast(FP8X4), rhs_scale=h_scales[:], start=True, stop=True,
+            )
+            y = sbuf(f"y{u}", [P, O], F32)
+            if u == 0:
+                nc.scalar.copy(y[:], y_ps[:])
+                nc.scalar.dma_start(out[rows, :], y[:])
+            else:
+                nc.vector.tensor_copy(y[:], y_ps[:])
+                nc.sync.dma_start(out[rows, :], y[:])

@@ -44,6 +44,11 @@ def tile_picked_largercode_store_one_pooledgroups_twobooks_plain_kernel(
         def fetch(dst, window, offsets, factor, t):
             nc.scalar.activation(dst, window[:].indirect(offsets), COPY, scale=factor[:, t : t + 1])
 
+        warm_in = sbuf("warm_in", [P, 1], F32)
+        warm_out = sbuf("warm_out", [P, 1], F32)
+        nc.vector.memset(warm_in[:], 0.0)
+        nc.scalar.activation(warm_out[:], warm_in[:], COPY)
+
         ta_w, tb_w, va_w, vb_w = [], [], [], []
         l1 = load_list("l1", offs)
         ga_t = load_factor(nc.scalar, "ga_t", ga)

@@ -53,33 +53,32 @@ def tile_picked_largercode_store_one_pooledgroups_twobooks_plain_kernel(
         l1 = load_list("l1", offs)
         ga_t = load_factor(nc.scalar, "ga_t", ga)
         gb_t = load_factor(nc.scalar, "gb_t", gb)
+        stage = sbuf("stage", [4, 4, F // 4], I32)
+        nc.gpsimd.dma_start(stage[:], wt_scales[0].bitcast(I32).rearrange("(q i) c -> i q c", i=4))
         ta_w.append(load_plane("ta", ta, 0))
         l2 = load_list("l2", offs2)
         tb_w.append(load_plane("tb", tb, 0))
-        stage = sbuf("stage", [4, 4, F // 4], I32)
-        nc.gpsimd.dma_start(stage[:], wt_scales[0].bitcast(I32).rearrange("(q i) c -> i q c", i=4))
-        ea_t = load_factor(nc.gpsimd, "ea_t", ea)
-        eb_t = load_factor(nc.gpsimd, "eb_t", eb)
-        sa_t = load_factor(nc.gpsimd, "sa_t", sa)
-        sb_t = load_factor(nc.gpsimd, "sb_t", sb)
-        for t in (1, 2):
-            ta_w.append(load_plane("ta", ta, t))
-            tb_w.append(load_plane("tb", tb, t))
         l3 = load_list("l3", offs3)
+        ta_w.append(load_plane("ta", ta, 1))
+        tb_w.append(load_plane("tb", tb, 1))
         words_w = sbuf("words_w", [P, F], U16)
         nc.sync.dma_start(words_w[:].bitcast(I32), wt_words[0].bitcast(I32))
-        ta_w.append(load_plane("ta", ta, 3))
-        tb_w.append(load_plane("tb", tb, 3))
+        for t in (2, 3):
+            ta_w.append(load_plane("ta", ta, t))
+            tb_w.append(load_plane("tb", tb, t))
         l6 = load_list("l6", offs6)
+        ea_t = load_factor(nc.sync, "ea_t", ea)
+        va_w.append(load_plane("va", va, 0))
         l7 = load_list("l7", offs7)
-        for t in (0, 1):
+        eb_t = load_factor(nc.sync, "eb_t", eb)
+        vb_w.append(load_plane("vb", vb, 0))
+        for t in (1, 2, 3):
             va_w.append(load_plane("va", va, t))
             vb_w.append(load_plane("vb", vb, t))
         l4 = load_list("l4", offs4)
+        sa_t = load_factor(nc.sync, "sa_t", sa)
         l5 = load_list("l5", offs5)
-        for t in (2, 3):
-            va_w.append(load_plane("va", va, t))
-            vb_w.append(load_plane("vb", vb, t))
+        sb_t = load_factor(nc.sync, "sb_t", sb)
 
         scales_w = sbuf("scales_w", [P, F], U8)
         nc.vector.memset(scales_w[:].bitcast(I32), 0)
@@ -110,8 +109,8 @@ def tile_picked_largercode_store_one_pooledgroups_twobooks_plain_kernel(
         x_scales = sbuf("x_scales", [P, J], U8)
         a_ps = [psum.tile([P, J], F32, name=f"a_ps{t}") for t in range(PACK)]
 
-        def weave(dst, in0, in1, op):
-            nc.vector.tensor_tensor(
+        def weave(engine, dst, in0, in1, op):
+            engine.tensor_tensor(
                 dst.rearrange("p (c i) t -> p c t i", i=2),
                 in0.rearrange("p t (c i) -> p c t i", i=2),
                 in1.rearrange("p t (c i) -> p c t i", i=2),
@@ -120,7 +119,7 @@ def tile_picked_largercode_store_one_pooledgroups_twobooks_plain_kernel(
 
         for h in range(2):
             cols = slice(h * H, (h + 1) * H)
-            weave(xc[:, cols, :], xa[:, :, cols], xb[:, :, cols], MAX)
+            weave(nc.vector, xc[:, cols, :], xa[:, :, cols], xb[:, :, cols], MAX)
             nc.vector.quantize_mx(
                 out=x_codes[:, cols].bitcast(FP8X4), scales=x_scales[:, cols],
                 in_=xc[:, cols, :].rearrange("p j t -> p (j t)"),
@@ -142,10 +141,11 @@ def tile_picked_largercode_store_one_pooledgroups_twobooks_plain_kernel(
         for t in range(PACK):
             fetch(ya[:, t, :], va_w[t], l6[:], ea_t, t)
             fetch(yb[:, t, :], vb_w[t], l7[:], eb_t, t)
-        vc = sbuf("vc", [P, N, PACK], BF16)
+        vc = sbuf("vc", [P, N, PACK], BF16, tag="xc")
         v_codes = sbuf("v_codes", [P, N], U32)
         v_scales = sbuf("v_scales", [P, N], U8)
-        weave(vc[:], ya[:], yb[:], ADD)
+        for planes in (slice(0, PACK - 1), slice(PACK - 1, PACK)):
+            weave(nc.gpsimd, vc[:, :, planes], ya[:, planes, :], yb[:, planes, :], ADD)
         nc.vector.quantize_mx(out=v_codes[:].bitcast(FP8X4), scales=v_scales[:], in_=vc[:].rearrange("p n t -> p (n t)"))
 
         hid = sbuf("hid", [P, O, PACK], BF16)

@@ -51,12 +51,12 @@ def tile_picked_largercode_store_one_pooledgroups_twobooks_plain_kernel(
 
         ta_w, tb_w, va_w, vb_w = [], [], [], []
         l1 = load_list("l1", offs)
-        ga_t = load_factor(nc.scalar, "ga_t", ga)
-        gb_t = load_factor(nc.scalar, "gb_t", gb)
+        ga_t = load_factor(nc.sync, "ga_t", ga)
         stage = sbuf("stage", [4, 4, F // 4], I32)
         nc.gpsimd.dma_start(stage[:], wt_scales[0].bitcast(I32).rearrange("(q i) c -> i q c", i=4))
         ta_w.append(load_plane("ta", ta, 0))
         l2 = load_list("l2", offs2)
+        gb_t = load_factor(nc.sync, "gb_t", gb)
         tb_w.append(load_plane("tb", tb, 0))
         l3 = load_list("l3", offs3)
         ta_w.append(load_plane("ta", ta, 1))
@@ -95,19 +95,19 @@ def tile_picked_largercode_store_one_pooledgroups_twobooks_plain_kernel(
 
         xa = sbuf("xa", [P, PACK, J], F32)
         xb = sbuf("xb", [P, PACK, J], F32)
+        larger = sbuf("larger", [P, PACK, J], BF16)
         H = J // 2
-        for t in range(PACK):
+        halves = [slice(0, H), slice(H, J)]
+        last = PACK - 1
+        for t in range(last):
             fetch(xa[:, t, :], ta_w[t], l1[:], ga_t, t)
-            if t < PACK - 1:
-                fetch(xb[:, t, :], tb_w[t], l2[:], gb_t, t)
-            else:
-                for h in range(2):
-                    fetch(xb[:, t, h * H : (h + 1) * H], tb_w[t], l2[:, h * H // 16 : (h + 1) * H // 16], gb_t, t)
+            fetch(xb[:, t, :], tb_w[t], l2[:], gb_t, t)
+            nc.vector.tensor_tensor(larger[:, t, :], xa[:, t, :], xb[:, t, :], MAX)
+        fetch(xa[:, last, :], ta_w[last], l1[:], ga_t, last)
 
         xc = sbuf("xc", [P, J, PACK], BF16)
         x_codes = sbuf("x_codes", [P, J], U32)
         x_scales = sbuf("x_scales", [P, J], U8)
-        a_ps = [psum.tile([P, J], F32, name=f"a_ps{t}") for t in range(PACK)]
 
         def weave(engine, dst, in0, in1, op):
             engine.tensor_tensor(
@@ -117,24 +117,35 @@ def tile_picked_largercode_store_one_pooledgroups_twobooks_plain_kernel(
                 op,
             )
 
-        for h in range(2):
-            cols = slice(h * H, (h + 1) * H)
-            weave(nc.vector, xc[:, cols, :], xa[:, :, cols], xb[:, :, cols], MAX)
+        def first_product(dst, t, cols):
+            nc.tensor.matmul_mx(
+                out=dst,
+                lhsT=w_words[:, t].rearrange("p m b -> p (m b)").bitcast(FP4X4),
+                lhsT_scale=w_scales[:, t, :],
+                rhs=x_codes[:, cols].bitcast(FP8X4), rhs_scale=x_scales[:, cols],
+                start=True, stop=True,
+            )
+
+        a_w = [sbuf(f"a_w{t}", [P, J], F32) for t in range(PACK)]
+        for h, cols in enumerate(halves):
+            fetch(xb[:, last, cols], tb_w[last], l2[:, cols.start // 16 : cols.stop // 16], gb_t, last)
+            nc.vector.tensor_tensor(larger[:, last, cols], xa[:, last, cols], xb[:, last, cols], MAX)
+            nc.vector.tensor_copy(
+                xc[:, cols, :].rearrange("p (c i) t -> p c t i", i=4),
+                larger[:, :, cols].rearrange("p t (c i) -> p c t i", i=4),
+            )
             nc.vector.quantize_mx(
                 out=x_codes[:, cols].bitcast(FP8X4), scales=x_scales[:, cols],
                 in_=xc[:, cols, :].rearrange("p j t -> p (j t)"),
             )
-        for t in range(PACK):
-            nc.tensor.matmul_mx(
-                out=a_ps[t][:],
-                lhsT=w_words[:, t].rearrange("p m b -> p (m b)").bitcast(FP4X4),
-                lhsT_scale=w_scales[:, t, :],
-                rhs=x_codes[:].bitcast(FP8X4), rhs_scale=x_scales[:],
-                start=True, stop=True,
-            )
-        a_w = [sbuf(f"a_w{t}", [P, J], F32) for t in range(PACK)]
-        for t in range(PACK):
-            nc.vector.tensor_copy(a_w[t][:], a_ps[t][:])
+        for h, cols in enumerate(halves):
+            half_ps = psum.tile([P, H], F32, name=f"half_ps{h}")
+            first_product(half_ps[:], 0, cols)
+            nc.vector.tensor_copy(a_w[0][:, cols], half_ps[:])
+        for t in range(1, PACK):
+            a_ps = psum.tile([P, J], F32, name=f"a_ps{t}")
+            first_product(a_ps[:], t, slice(0, J))
+            nc.vector.tensor_copy(a_w[t][:], a_ps[:])
 
         ya = sbuf("ya", [P, PACK, N], F32)
         yb = sbuf("yb", [P, PACK, N], F32)
@@ -153,7 +164,7 @@ def tile_picked_largercode_store_one_pooledgroups_twobooks_plain_kernel(
         for t in range(PACK):
             both = picks[:, t]
             fetch(both[:, 0, :], a_w[t], l4[:], sa_t, t)
-            cuts = (0, S) if t < PACK - 1 else (0, S - 64, S)
+            cuts = (0, S) if t < PACK - 1 else (0, S // 2, S)
             for s0, s1 in zip(cuts, cuts[1:]):
                 fetch(both[:, 1, s0:s1], a_w[t], l5[:, s0 // 16 : s1 // 16], sb_t, t)
                 nc.vector.tensor_reduce(

@@ -2,11 +2,16 @@ from contextlib import ExitStack
 
 import concourse.mybir as mybir
 
-K, J, R, T, F, S, O, N, Z = 512, 512, 512, 1024, 1024, 256, 128, 256, 512
+K, J, R, F, S, O, N = 512, 512, 512, 1024, 256, 128, 256
 FLOPS = 2 * K * R * J + 2 * R * N * O
 
 P = 128
 PACK = 4
+LAST = PACK - 1
+PER_COLUMN = 16
+QUADRANTS, SCALE_ROWS = 4, 4
+POOL = S // O
+
 F32, BF16 = mybir.dt.float32, mybir.dt.bfloat16
 I32, U32, U16, U8 = mybir.dt.int32, mybir.dt.uint32, mybir.dt.uint16, mybir.dt.uint8
 FP8X4, FP4X4 = mybir.dt.float8_e4m3fn_x4, mybir.dt.float4_e2m1fn_x4
@@ -31,9 +36,9 @@ def tile_picked_largercode_store_one_pooledgroups_twobooks_plain_kernel(
             nc.sync.dma_start(tile[:], src)
             return tile
 
-        def load_factor(queue, name, src):
+        def load_factor(name, src):
             tile = sbuf(name, [P, PACK], F32)
-            queue.dma_start(tile[:], src.rearrange("(p t) o -> p (t o)", t=PACK))
+            nc.sync.dma_start(tile[:], src.rearrange("(p t) o -> p (t o)", t=PACK))
             return tile
 
         def load_plane(name, src, t):
@@ -44,148 +49,141 @@ def tile_picked_largercode_store_one_pooledgroups_twobooks_plain_kernel(
         def fetch(dst, window, offsets, factor, t):
             nc.scalar.activation(dst, window[:].indirect(offsets), COPY, scale=factor[:, t : t + 1])
 
+        def entries(list_tile, span):
+            return list_tile[:, span.start // PER_COLUMN : span.stop // PER_COLUMN]
+
+        def halves(n):
+            return slice(0, n // 2), slice(n // 2, n)
+
         warm_in = sbuf("warm_in", [P, 1], F32)
         warm_out = sbuf("warm_out", [P, 1], F32)
         nc.vector.memset(warm_in[:], 0.0)
         nc.scalar.activation(warm_out[:], warm_in[:], COPY)
 
-        ta_w, tb_w, va_w, vb_w = [], [], [], []
-        l1 = load_list("l1", offs)
-        ga_t = load_factor(nc.sync, "ga_t", ga)
-        stage = sbuf("stage", [4, 4, F // 4], I32)
-        nc.gpsimd.dma_start(stage[:], wt_scales[0].bitcast(I32).rearrange("(q i) c -> i q c", i=4))
-        ta_w.append(load_plane("ta", ta, 0))
-        l2 = load_list("l2", offs2)
-        gb_t = load_factor(nc.sync, "gb_t", gb)
-        tb_w.append(load_plane("tb", tb, 0))
-        l3 = load_list("l3", offs3)
-        ta_w.append(load_plane("ta", ta, 1))
-        tb_w.append(load_plane("tb", tb, 1))
-        words_w = sbuf("words_w", [P, F], U16)
-        nc.sync.dma_start(words_w[:].bitcast(I32), wt_words[0].bitcast(I32))
-        for t in (2, 3):
-            ta_w.append(load_plane("ta", ta, t))
-            tb_w.append(load_plane("tb", tb, t))
-        l6 = load_list("l6", offs6)
-        ea_t = load_factor(nc.sync, "ea_t", ea)
-        va_w.append(load_plane("va", va, 0))
-        l7 = load_list("l7", offs7)
-        eb_t = load_factor(nc.sync, "eb_t", eb)
-        vb_w.append(load_plane("vb", vb, 0))
-        for t in (1, 2, 3):
-            va_w.append(load_plane("va", va, t))
-            vb_w.append(load_plane("vb", vb, t))
-        l4 = load_list("l4", offs4)
-        sa_t = load_factor(nc.sync, "sa_t", sa)
-        l5 = load_list("l5", offs5)
-        sb_t = load_factor(nc.sync, "sb_t", sb)
+        ta_planes, tb_planes, va_planes, vb_planes = [], [], [], []
+        ta_list = load_list("ta_list", offs)
+        ga_cols = load_factor("ga_cols", ga)
+        scale_stage = sbuf("scale_stage", [SCALE_ROWS, QUADRANTS, F // 4], I32)
+        nc.gpsimd.dma_start(scale_stage[:], wt_scales[0].bitcast(I32).rearrange("(q i) c -> i q c", i=SCALE_ROWS))
+        ta_planes.append(load_plane("ta", ta, 0))
+        tb_list = load_list("tb_list", offs2)
+        gb_cols = load_factor("gb_cols", gb)
+        tb_planes.append(load_plane("tb", tb, 0))
+        wt_list = load_list("wt_list", offs3)
+        for t in range(1, PACK):
+            ta_planes.append(load_plane("ta", ta, t))
+            tb_planes.append(load_plane("tb", tb, t))
+        words_window = sbuf("words_window", [P, F], U16)
+        nc.sync.dma_start(words_window[:].bitcast(I32), wt_words[0].bitcast(I32))
+        va_list = load_list("va_list", offs6)
+        ea_cols = load_factor("ea_cols", ea)
+        va_planes.append(load_plane("va", va, 0))
+        vb_list = load_list("vb_list", offs7)
+        eb_cols = load_factor("eb_cols", eb)
+        vb_planes.append(load_plane("vb", vb, 0))
+        for t in range(1, PACK):
+            va_planes.append(load_plane("va", va, t))
+            vb_planes.append(load_plane("vb", vb, t))
+        group_list = load_list("group_list", offs4)
+        sa_cols = load_factor("sa_cols", sa)
+        shared_list = load_list("shared_list", offs5)
+        sb_cols = load_factor("sb_cols", sb)
 
-        scales_w = sbuf("scales_w", [P, F], U8)
-        nc.vector.memset(scales_w[:].bitcast(I32), 0)
-        for q in range(4):
-            nc.vector.tensor_copy(scales_w[32 * q : 32 * q + 4, :].bitcast(I32), stage[:, q, :])
+        scales_window = sbuf("scales_window", [P, F], U8)
+        nc.vector.memset(scales_window[:].bitcast(I32), 0)
+        for q in range(QUADRANTS):
+            nc.vector.tensor_copy(scales_window[32 * q : 32 * q + SCALE_ROWS, :].bitcast(I32), scale_stage[:, q, :])
         w_scales = sbuf("w_scales", [P, PACK, P], U8)
-        nc.vector.tensor_copy(w_scales[:].rearrange("p t m -> p m t"), scales_w[:].indirect(l3[:]))
-        picked = sbuf("picked", [P, R], U16)
-        nc.vector.tensor_copy(picked[:], words_w[:].indirect(l3[:]))
+        nc.vector.tensor_copy(w_scales[:].rearrange("p t m -> p m t"), scales_window[:].indirect(wt_list[:]))
+        picked_words = sbuf("picked_words", [P, R], U16)
+        nc.vector.tensor_copy(picked_words[:], words_window[:].indirect(wt_list[:]))
         w_words = sbuf("w_words", [P, PACK, P, 2], U8)
-        nc.vector.tensor_copy(
-            w_words[:], picked[:].bitcast(U8).rearrange("p (m t b) -> p t m b", t=PACK, b=2)
-        )
+        words_by_tile = picked_words[:].bitcast(U8).rearrange("p (m t b) -> p t m b", t=PACK, b=2)
+        nc.vector.tensor_copy(w_words[:, 0], words_by_tile[:, 0])
 
-        xa = sbuf("xa", [P, PACK, J], F32)
-        xb = sbuf("xb", [P, PACK, J], F32)
-        larger = sbuf("larger", [P, PACK, J], BF16)
-        H = J // 2
-        halves = [slice(0, H), slice(H, J)]
-        last = PACK - 1
-        for t in range(last):
-            fetch(xa[:, t, :], ta_w[t], l1[:], ga_t, t)
-            fetch(xb[:, t, :], tb_w[t], l2[:], gb_t, t)
-            nc.vector.tensor_tensor(larger[:, t, :], xa[:, t, :], xb[:, t, :], MAX)
-        fetch(xa[:, last, :], ta_w[last], l1[:], ga_t, last)
+        ta_scaled = sbuf("ta_scaled", [P, PACK, J], F32)
+        tb_scaled = sbuf("tb_scaled", [P, PACK, J], F32)
+        xc_planes = sbuf("xc_planes", [P, PACK, J], BF16)
+        for t in range(LAST):
+            fetch(ta_scaled[:, t, :], ta_planes[t], ta_list[:], ga_cols, t)
+            fetch(tb_scaled[:, t, :], tb_planes[t], tb_list[:], gb_cols, t)
+            nc.vector.tensor_tensor(xc_planes[:, t, :], ta_scaled[:, t, :], tb_scaled[:, t, :], MAX)
+        fetch(ta_scaled[:, LAST, :], ta_planes[LAST], ta_list[:], ga_cols, LAST)
 
         xc = sbuf("xc", [P, J, PACK], BF16)
         x_codes = sbuf("x_codes", [P, J], U32)
         x_scales = sbuf("x_scales", [P, J], U8)
+        a_planes = [sbuf(f"a{t}", [P, J], F32) for t in range(PACK)]
 
-        def weave(engine, dst, in0, in1, op):
-            engine.tensor_tensor(
-                dst.rearrange("p (c i) t -> p c t i", i=2),
-                in0.rearrange("p t (c i) -> p c t i", i=2),
-                in1.rearrange("p t (c i) -> p c t i", i=2),
-                op,
-            )
-
-        def first_product(dst, t, cols):
+        def first_product(dst, t, slots):
             nc.tensor.matmul_mx(
                 out=dst,
-                lhsT=w_words[:, t].rearrange("p m b -> p (m b)").bitcast(FP4X4),
-                lhsT_scale=w_scales[:, t, :],
-                rhs=x_codes[:, cols].bitcast(FP8X4), rhs_scale=x_scales[:, cols],
+                lhsT=w_words[:, t].rearrange("p m b -> p (m b)").bitcast(FP4X4), lhsT_scale=w_scales[:, t, :],
+                rhs=x_codes[:, slots].bitcast(FP8X4), rhs_scale=x_scales[:, slots],
                 start=True, stop=True,
             )
 
-        a_w = [sbuf(f"a_w{t}", [P, J], F32) for t in range(PACK)]
-        for h, cols in enumerate(halves):
-            fetch(xb[:, last, cols], tb_w[last], l2[:, cols.start // 16 : cols.stop // 16], gb_t, last)
-            nc.vector.tensor_tensor(larger[:, last, cols], xa[:, last, cols], xb[:, last, cols], MAX)
+        for slots in halves(J):
+            fetch(tb_scaled[:, LAST, slots], tb_planes[LAST], entries(tb_list, slots), gb_cols, LAST)
+            nc.vector.tensor_tensor(xc_planes[:, LAST, slots], ta_scaled[:, LAST, slots], tb_scaled[:, LAST, slots], MAX)
             nc.vector.tensor_copy(
-                xc[:, cols, :].rearrange("p (c i) t -> p c t i", i=4),
-                larger[:, :, cols].rearrange("p t (c i) -> p c t i", i=4),
+                xc[:, slots, :].rearrange("p (c i) t -> p c t i", i=4),
+                xc_planes[:, :, slots].rearrange("p t (c i) -> p c t i", i=4),
             )
             nc.vector.quantize_mx(
-                out=x_codes[:, cols].bitcast(FP8X4), scales=x_scales[:, cols],
-                in_=xc[:, cols, :].rearrange("p j t -> p (j t)"),
+                out=x_codes[:, slots].bitcast(FP8X4), scales=x_scales[:, slots],
+                in_=xc[:, slots, :].rearrange("p j t -> p (j t)"),
             )
-        for h, cols in enumerate(halves):
-            half_ps = psum.tile([P, H], F32, name=f"half_ps{h}")
-            first_product(half_ps[:], 0, cols)
-            nc.vector.tensor_copy(a_w[0][:, cols], half_ps[:])
+        for h, slots in enumerate(halves(J)):
+            half_bank = psum.tile([P, J // 2], F32, name=f"half_bank{h}")
+            first_product(half_bank[:], 0, slots)
+            nc.vector.tensor_copy(a_planes[0][:, slots], half_bank[:])
+        nc.vector.tensor_copy(w_words[:, 1:PACK], words_by_tile[:, 1:PACK])
         for t in range(1, PACK):
-            a_ps = psum.tile([P, J], F32, name=f"a_ps{t}")
-            first_product(a_ps[:], t, slice(0, J))
-            nc.vector.tensor_copy(a_w[t][:], a_ps[:])
+            a_bank = psum.tile([P, J], F32, name=f"a_bank{t}")
+            first_product(a_bank[:], t, slice(0, J))
+            nc.vector.tensor_copy(a_planes[t][:], a_bank[:])
 
-        ya = sbuf("ya", [P, PACK, N], F32)
-        yb = sbuf("yb", [P, PACK, N], F32)
+        va_scaled = sbuf("va_scaled", [P, PACK, N], F32)
+        vb_scaled = sbuf("vb_scaled", [P, PACK, N], F32)
         for t in range(PACK):
-            fetch(ya[:, t, :], va_w[t], l6[:], ea_t, t)
-            fetch(yb[:, t, :], vb_w[t], l7[:], eb_t, t)
+            fetch(va_scaled[:, t, :], va_planes[t], va_list[:], ea_cols, t)
+            fetch(vb_scaled[:, t, :], vb_planes[t], vb_list[:], eb_cols, t)
         vc = sbuf("vc", [P, N, PACK], BF16, tag="xc")
         v_codes = sbuf("v_codes", [P, N], U32)
         v_scales = sbuf("v_scales", [P, N], U8)
-        for planes in (slice(0, PACK - 1), slice(PACK - 1, PACK)):
-            weave(nc.gpsimd, vc[:, :, planes], ya[:, planes, :], yb[:, planes, :], ADD)
+        for planes in (slice(0, LAST), slice(LAST, PACK)):
+            nc.gpsimd.tensor_tensor(
+                vc[:, :, planes].rearrange("p (c i) t -> p c t i", i=2),
+                va_scaled[:, planes, :].rearrange("p t (c i) -> p c t i", i=2),
+                vb_scaled[:, planes, :].rearrange("p t (c i) -> p c t i", i=2),
+                ADD,
+            )
         nc.vector.quantize_mx(out=v_codes[:].bitcast(FP8X4), scales=v_scales[:], in_=vc[:].rearrange("p n t -> p (n t)"))
 
         hid = sbuf("hid", [P, O, PACK], BF16)
-        picks = sbuf("picks", [P, PACK, 2, S], F32, tag="vb3")
+        a_scaled = sbuf("a_scaled", [P, PACK, 2, S], F32)
         for t in range(PACK):
-            both = picks[:, t]
-            fetch(both[:, 0, :], a_w[t], l4[:], sa_t, t)
-            cuts = (0, S) if t < PACK - 1 else (0, S // 2, S)
-            for s0, s1 in zip(cuts, cuts[1:]):
-                fetch(both[:, 1, s0:s1], a_w[t], l5[:, s0 // 16 : s1 // 16], sb_t, t)
+            fetch(a_scaled[:, t, 0, :], a_planes[t], group_list[:], sa_cols, t)
+            for picks in halves(S) if t == LAST else (slice(0, S),):
+                fetch(a_scaled[:, t, 1, picks], a_planes[t], entries(shared_list, picks), sb_cols, t)
                 nc.vector.tensor_reduce(
-                    hid[:, s0 // 2 : s1 // 2, t], both[:, :, s0:s1].rearrange("p l (o d) -> p o l d", d=2),
+                    hid[:, picks.start // POOL : picks.stop // POOL, t],
+                    a_scaled[:, t, :, picks].rearrange("p l (o d) -> p o l d", d=POOL),
                     mybir.AxisListType.XY, MAX,
                 )
         h_codes = sbuf("h_codes", [P, O], U32)
         h_scales = sbuf("h_scales", [P, O], U8)
         nc.vector.quantize_mx(out=h_codes[:].bitcast(FP8X4), scales=h_scales[:], in_=hid[:].rearrange("p o t -> p (o t)"))
 
-        for u in range(N // P):
+        ways_out = ((nc.scalar.copy, nc.scalar), (nc.vector.tensor_copy, nc.sync))
+        for u, (copy_out, queue) in enumerate(ways_out):
             rows = slice(u * P, (u + 1) * P)
-            y_ps = psum.tile([P, O], F32, name=f"y_ps{u}")
+            out_bank = psum.tile([P, O], F32, name=f"out_bank{u}")
             nc.tensor.matmul_mx(
-                out=y_ps[:], lhsT=v_codes[:, rows].bitcast(FP8X4), lhsT_scale=v_scales[:, rows],
+                out=out_bank[:], lhsT=v_codes[:, rows].bitcast(FP8X4), lhsT_scale=v_scales[:, rows],
                 rhs=h_codes[:].bitcast(FP8X4), rhs_scale=h_scales[:], start=True, stop=True,
             )
-            y = sbuf(f"y{u}", [P, O], F32)
-            if u == 0:
-                nc.scalar.copy(y[:], y_ps[:])
-                nc.scalar.dma_start(out[rows, :], y[:])
-            else:
-                nc.vector.tensor_copy(y[:], y_ps[:])
-                nc.sync.dma_start(out[rows, :], y[:])
+            result = sbuf(f"result{u}", [P, O], F32)
+            copy_out(result[:], out_bank[:])
+            queue.dma_start(out[rows, :], result[:])

from contextlib import ExitStack

import concourse.mybir as mybir

K, J, R, F, S, O, N = 512, 512, 512, 1024, 256, 128, 256
FLOPS = 2 * K * R * J + 2 * R * N * O

P = 128
PACK = 4
LAST = PACK - 1
PER_COLUMN = 16
QUADRANTS, SCALE_ROWS = 4, 4
POOL = S // O

F32, BF16 = mybir.dt.float32, mybir.dt.bfloat16
I32, U32, U16, U8 = mybir.dt.int32, mybir.dt.uint32, mybir.dt.uint16, mybir.dt.uint8
FP8X4, FP4X4 = mybir.dt.float8_e4m3fn_x4, mybir.dt.float4_e2m1fn_x4
COPY = mybir.ActivationFunctionType.Copy
MAX, ADD = mybir.AluOpType.max, mybir.AluOpType.add


def tile_picked_largercode_store_one_pooledgroups_twobooks_plain_kernel(
    tc, ta, tb, ga, gb, wt_words, wt_scales, sa, sb, va, vb, ea, eb,
    offs, offs2, offs3, offs4, offs5, offs6, offs7, out,
):
    nc = tc.nc
    with ExitStack() as ctx:
        keep = ctx.enter_context(tc.tile_pool(name="keep", bufs=1))
        psum = ctx.enter_context(tc.psum_pool(name="psum", bufs=1))

        def sbuf(name, shape, dtype, tag=None):
            return keep.tile(shape, dtype, name=name, tag=tag or name, align_bytes=64)

        def load_list(name, src):
            tile = sbuf(name, list(src.shape), U16)
            nc.sync.dma_start(tile[:], src)
            return tile

        def load_factor(name, src):
            tile = sbuf(name, [P, PACK], F32)
            nc.sync.dma_start(tile[:], src.rearrange("(p t) o -> p (t o)", t=PACK))
            return tile

        def load_plane(name, src, t):
            tile = sbuf(f"{name}{t}", [P, src.shape[1]], F32)
            nc.sync.dma_start(tile[:], src.rearrange("(p t) c -> p t c", t=PACK)[:, t, :])
            return tile

        def fetch(dst, window, offsets, factor, t):
            nc.scalar.activation(dst, window[:].indirect(offsets), COPY, scale=factor[:, t : t + 1])

        def entries(list_tile, span):
            return list_tile[:, span.start // PER_COLUMN : span.stop // PER_COLUMN]

        def halves(n):
            return slice(0, n // 2), slice(n // 2, n)

        warm_in = sbuf("warm_in", [P, 1], F32)
        warm_out = sbuf("warm_out", [P, 1], F32)
        nc.vector.memset(warm_in[:], 0.0)
        nc.scalar.activation(warm_out[:], warm_in[:], COPY)

        ta_planes, tb_planes, va_planes, vb_planes = [], [], [], []
        ta_list = load_list("ta_list", offs)
        ga_cols = load_factor("ga_cols", ga)
        scale_stage = sbuf("scale_stage", [SCALE_ROWS, QUADRANTS, F // 4], I32)
        nc.gpsimd.dma_start(scale_stage[:], wt_scales[0].bitcast(I32).rearrange("(q i) c -> i q c", i=SCALE_ROWS))
        ta_planes.append(load_plane("ta", ta, 0))
        tb_list = load_list("tb_list", offs2)
        gb_cols = load_factor("gb_cols", gb)
        tb_planes.append(load_plane("tb", tb, 0))
        wt_list = load_list("wt_list", offs3)
        for t in range(1, PACK):
            ta_planes.append(load_plane("ta", ta, t))
            tb_planes.append(load_plane("tb", tb, t))
        words_window = sbuf("words_window", [P, F], U16)
        nc.sync.dma_start(words_window[:].bitcast(I32), wt_words[0].bitcast(I32))
        va_list = load_list("va_list", offs6)
        ea_cols = load_factor("ea_cols", ea)
        va_planes.append(load_plane("va", va, 0))
        vb_list = load_list("vb_list", offs7)
        eb_cols = load_factor("eb_cols", eb)
        vb_planes.append(load_plane("vb", vb, 0))
        for t in range(1, PACK):
            va_planes.append(load_plane("va", va, t))
            vb_planes.append(load_plane("vb", vb, t))
        group_list = load_list("group_list", offs4)
        sa_cols = load_factor("sa_cols", sa)
        shared_list = load_list("shared_list", offs5)
        sb_cols = load_factor("sb_cols", sb)

        scales_window = sbuf("scales_window", [P, F], U8)
        nc.vector.memset(scales_window[:].bitcast(I32), 0)
        for q in range(QUADRANTS):
            nc.vector.tensor_copy(scales_window[32 * q : 32 * q + SCALE_ROWS, :].bitcast(I32), scale_stage[:, q, :])
        w_scales = sbuf("w_scales", [P, PACK, P], U8)
        nc.vector.tensor_copy(w_scales[:].rearrange("p t m -> p m t"), scales_window[:].indirect(wt_list[:]))
        picked_words = sbuf("picked_words", [P, R], U16)
        nc.vector.tensor_copy(picked_words[:], words_window[:].indirect(wt_list[:]))
        w_words = sbuf("w_words", [P, PACK, P, 2], U8)
        words_by_tile = picked_words[:].bitcast(U8).rearrange("p (m t b) -> p t m b", t=PACK, b=2)
        nc.vector.tensor_copy(w_words[:, 0], words_by_tile[:, 0])

        ta_scaled = sbuf("ta_scaled", [P, PACK, J], F32)
        tb_scaled = sbuf("tb_scaled", [P, PACK, J], F32)
        xc_planes = sbuf("xc_planes", [P, PACK, J], BF16)
        for t in range(LAST):
            fetch(ta_scaled[:, t, :], ta_planes[t], ta_list[:], ga_cols, t)
            fetch(tb_scaled[:, t, :], tb_planes[t], tb_list[:], gb_cols, t)
            nc.vector.tensor_tensor(xc_planes[:, t, :], ta_scaled[:, t, :], tb_scaled[:, t, :], MAX)
        fetch(ta_scaled[:, LAST, :], ta_planes[LAST], ta_list[:], ga_cols, LAST)

        xc = sbuf("xc", [P, J, PACK], BF16)
        x_codes = sbuf("x_codes", [P, J], U32)
        x_scales = sbuf("x_scales", [P, J], U8)
        a_planes = [sbuf(f"a{t}", [P, J], F32) for t in range(PACK)]

        def first_product(dst, t, slots):
            nc.tensor.matmul_mx(
                out=dst,
                lhsT=w_words[:, t].rearrange("p m b -> p (m b)").bitcast(FP4X4), lhsT_scale=w_scales[:, t, :],
                rhs=x_codes[:, slots].bitcast(FP8X4), rhs_scale=x_scales[:, slots],
                start=True, stop=True,
            )

        for slots in halves(J):
            fetch(tb_scaled[:, LAST, slots], tb_planes[LAST], entries(tb_list, slots), gb_cols, LAST)
            nc.vector.tensor_tensor(xc_planes[:, LAST, slots], ta_scaled[:, LAST, slots], tb_scaled[:, LAST, slots], MAX)
            nc.vector.tensor_copy(
                xc[:, slots, :].rearrange("p (c i) t -> p c t i", i=4),
                xc_planes[:, :, slots].rearrange("p t (c i) -> p c t i", i=4),
            )
            nc.vector.quantize_mx(
                out=x_codes[:, slots].bitcast(FP8X4), scales=x_scales[:, slots],
                in_=xc[:, slots, :].rearrange("p j t -> p (j t)"),
            )
        for h, slots in enumerate(halves(J)):
            half_bank = psum.tile([P, J // 2], F32, name=f"half_bank{h}")
            first_product(half_bank[:], 0, slots)
            nc.vector.tensor_copy(a_planes[0][:, slots], half_bank[:])
        nc.vector.tensor_copy(w_words[:, 1:PACK], words_by_tile[:, 1:PACK])
        for t in range(1, PACK):
            a_bank = psum.tile([P, J], F32, name=f"a_bank{t}")
            first_product(a_bank[:], t, slice(0, J))
            nc.vector.tensor_copy(a_planes[t][:], a_bank[:])

        va_scaled = sbuf("va_scaled", [P, PACK, N], F32)
        vb_scaled = sbuf("vb_scaled", [P, PACK, N], F32)
        for t in range(PACK):
            fetch(va_scaled[:, t, :], va_planes[t], va_list[:], ea_cols, t)
            fetch(vb_scaled[:, t, :], vb_planes[t], vb_list[:], eb_cols, t)
        vc = sbuf("vc", [P, N, PACK], BF16, tag="xc")
        v_codes = sbuf("v_codes", [P, N], U32)
        v_scales = sbuf("v_scales", [P, N], U8)
        for planes in (slice(0, LAST), slice(LAST, PACK)):
            nc.gpsimd.tensor_tensor(
                vc[:, :, planes].rearrange("p (c i) t -> p c t i", i=2),
                va_scaled[:, planes, :].rearrange("p t (c i) -> p c t i", i=2),
                vb_scaled[:, planes, :].rearrange("p t (c i) -> p c t i", i=2),
                ADD,
            )
        nc.vector.quantize_mx(out=v_codes[:].bitcast(FP8X4), scales=v_scales[:], in_=vc[:].rearrange("p n t -> p (n t)"))

        hid = sbuf("hid", [P, O, PACK], BF16)
        a_scaled = sbuf("a_scaled", [P, PACK, 2, S], F32)
        for t in range(PACK):
            fetch(a_scaled[:, t, 0, :], a_planes[t], group_list[:], sa_cols, t)
            for picks in halves(S) if t == LAST else (slice(0, S),):
                fetch(a_scaled[:, t, 1, picks], a_planes[t], entries(shared_list, picks), sb_cols, t)
                nc.vector.tensor_reduce(
                    hid[:, picks.start // POOL : picks.stop // POOL, t],
                    a_scaled[:, t, :, picks].rearrange("p l (o d) -> p o l d", d=POOL),
                    mybir.AxisListType.XY, MAX,
                )
        h_codes = sbuf("h_codes", [P, O], U32)
        h_scales = sbuf("h_scales", [P, O], U8)
        nc.vector.quantize_mx(out=h_codes[:].bitcast(FP8X4), scales=h_scales[:], in_=hid[:].rearrange("p o t -> p (o t)"))

        ways_out = ((nc.scalar.copy, nc.scalar), (nc.vector.tensor_copy, nc.sync))
        for u, (copy_out, queue) in enumerate(ways_out):
            rows = slice(u * P, (u + 1) * P)
            out_bank = psum.tile([P, O], F32, name=f"out_bank{u}")
            nc.tensor.matmul_mx(
                out=out_bank[:], lhsT=v_codes[:, rows].bitcast(FP8X4), lhsT_scale=v_scales[:, rows],
                rhs=h_codes[:].bitcast(FP8X4), rhs_scale=h_scales[:], start=True, stop=True,
            )
            result = sbuf(f"result{u}", [P, O], F32)
            copy_out(result[:], out_bank[:])
            queue.dma_start(out[rows, :], result[:])
